import numpy as np
import ml_dtypes


def mxq(x, axis, fmt="e4m3"):
    dtype, down = {"e4m3": (ml_dtypes.float8_e4m3fn, 7), "e5m2": (ml_dtypes.float8_e5m2, 14)}[fmt]
    v = np.moveaxis(np.asarray(x, np.float32).astype(ml_dtypes.bfloat16).astype(np.float64), axis, -1)
    blocks = v.reshape(v.shape[:-1] + (-1, 32))
    amax = np.abs(blocks).max(-1, keepdims=True)
    byte = np.maximum(np.where(amax > 0, np.frexp(amax)[1] - 1 + 127, 0) - down, 1)
    scale = np.exp2(byte - 127.0)
    codes = (blocks / scale).astype(np.float32).astype(dtype).astype(np.float64)
    return np.moveaxis((codes * scale).reshape(v.shape), -1, axis)


WIDE = False


def mx_kscale(k):
    if not WIDE:
        return np.ones(k)
    levels = np.array([30, -30])
    if k % 512:
        return np.exp2(np.random.permutation(np.resize(levels, k // 32))).repeat(32)
    a = np.empty((k // 512, 16))
    for p in range(k // 512):
        a[p, :8] = np.random.permutation(np.resize(levels, 8))
        for g in range(8):
            far = levels[np.abs(levels - a[p, g]) >= 10]
            a[p, g + 8] = far[np.random.randint(len(far))]
    return np.exp2(a.ravel()).repeat(32)


def f64(x):
    return np.asarray(x).astype(np.float64)


E2M1 = np.array([0.0, 0.5, 1.0, 1.5, 2.0, 3.0, 4.0, 6.0, -0.0, -0.5, -1.0, -1.5, -2.0, -3.0, -4.0, -6.0])


def pack_weight(w, fmt):
    k, n = w.shape
    w = f64(np.asarray(w, np.float32).astype(ml_dtypes.bfloat16)).reshape(k // 32, 32, n)
    amax = np.abs(w).max(1)
    if fmt == "e4m3":
        byte = np.frexp(amax)[1] - 1 + 127 - 7
    else:
        mant, ex = np.frexp(amax / 6.0)
        byte = np.where(mant > 0.5, ex, ex - 1) + 127
    byte = np.clip(np.where(amax > 0, byte, 1), 1, 254)
    scaled = (w * np.exp2(127.0 - byte)[:, None, :]).reshape(k, n).astype(np.float32)
    by_word = np.ascontiguousarray(scaled.reshape(k // 512, 128, 4, n).transpose(0, 1, 3, 2))
    if fmt == "e4m3":
        words = by_word.astype(ml_dtypes.float8_e4m3fn).view(np.uint8)
    else:
        c = by_word.astype(ml_dtypes.float4_e2m1fn).view(np.uint8) & 0xF
        words = (c[..., 0::2] | (c[..., 1::2] << 4)).reshape(k // 512, 128, 2 * n)
    return np.ascontiguousarray(words), np.ascontiguousarray(byte.astype(np.uint8).reshape(k // 512, 16, n))


def unpack_weight(words, scales, fmt):
    g, _, n = scales.shape
    words = np.ascontiguousarray(words).reshape(g, 128, n, -1)
    if fmt == "e4m3":
        vals = words.view(ml_dtypes.float8_e4m3fn).astype(np.float64)
    else:
        nib = np.empty((g, 128, n, 4), np.uint8)
        nib[..., 0::2] = words & 0xF
        nib[..., 1::2] = words >> 4
        vals = E2M1[nib]
    vals = vals * np.repeat(np.exp2(scales.astype(np.float64) - 127.0), 8, axis=1)[..., None]
    return vals.transpose(0, 1, 3, 2).reshape(g * 512, n)


K, T, J, M, N = 512, 512, 512, 512, 512


def setup_inputs():
    n = np.random.standard_normal
    fk = mx_kscale(K)
    fj = mx_kscale(J)
    fm = mx_kscale(M)
    tq = np.exp(2 * n((T, J)))
    xtp = pack_weight(n((K, T)) * 0.4 / fk[:, None], "e4m3")
    wcp = pack_weight(n((K, J)) * 1 / np.sqrt(K) * fk[:, None], "e2m1")
    wop = pack_weight(n((J, N)) * 1 / np.sqrt(J) / fj[:, None], "e4m3")
    wrp = pack_weight(n((K, M)) * 1 / np.sqrt(K) * fk[:, None], "e2m1")
    wbp = pack_weight(n((M, N)) * 1 / np.sqrt(M) / fm[:, None], "e4m3")
    return {
        "xt_words": xtp[0],
        "xt_scales": xtp[1],
        "wc_words": wcp[0],
        "wc_scales": wcp[1],
        "tg": (tq / tq.sum(axis=1, keepdims=True)).astype(np.float32),
        "fj": (np.random.uniform(64.0, 128.0, (J, 1)) * fj[:, None]).astype(np.float32),
        "wo_words": wop[0],
        "wo_scales": wop[1],
        "wr_words": wrp[0],
        "wr_scales": wrp[1],
        "tr1": (1.0 * n((M, T))).astype(np.float32),
        "fm": (np.random.uniform(0.5, 2.0, (M, 1)) * fm[:, None]).astype(np.float32),
        "wb_words": wbp[0],
        "wb_scales": wbp[1],
    }


def reference(xt_words, xt_scales, wc_words, wc_scales, tg, fj, wo_words, wo_scales, wr_words, wr_scales, tr1, fm, wb_words, wb_scales):
    xtu = unpack_weight(xt_words, xt_scales, "e4m3")
    wcu = unpack_weight(wc_words, wc_scales, "e2m1")
    wou = unpack_weight(wo_words, wo_scales, "e4m3")
    wru = unpack_weight(wr_words, wr_scales, "e2m1")
    wbu = unpack_weight(wb_words, wb_scales, "e4m3")
    a = xtu.T @ wcu
    e = np.exp(a)
    d = e / np.sum(e, axis=1, keepdims=True) - f64(tg)
    dt1 = d.T
    dj = dt1 * f64(fj)
    r = wru.T @ xtu
    dm = (r - f64(tr1)) * f64(fm)
    djq = mxq(dj, 0, "e5m2")
    dmq = mxq(dm, 0, "e4m3")
    y = wou.T @ djq + wbu.T @ dmq
    return y

@@ -1,0 +1,276 @@
+from contextlib import ExitStack
+
+import concourse.mybir as mybir
+from concourse.masks import make_identity
+
+F32 = mybir.dt.float32
+BF16 = mybir.dt.bfloat16
+I32 = mybir.dt.int32
+U32 = mybir.dt.uint32
+U8 = mybir.dt.uint8
+E4M3 = mybir.dt.float8_e4m3fn_x4
+E5M2 = mybir.dt.float8_e5m2_x4
+E2M1 = mybir.dt.float4_e2m1fn_x4
+ALU = mybir.AluOpType
+ACT = mybir.ActivationFunctionType
+AX = mybir.AxisListType
+
+P = 128
+D = 512
+R = 4
+NT = D // P
+HALF = D // 2
+FLOPS = 4 * 2 * D * D * D
+
+
+def tile_mix_errors_of_two_heads_back_kernel(
+    tc, xt_words, xt_scales, wc_words, wc_scales, tg, fj, wo_words, wo_scales,
+    wr_words, wr_scales, tr1, fm, wb_words, wb_scales, out,
+):
+    nc = tc.nc
+    with ExitStack() as ctx:
+        sb = ctx.enter_context(tc.tile_pool(name="sb", bufs=1))
+        ps = ctx.enter_context(tc.psum_pool(name="ps", bufs=1))
+        ctx.enter_context(tc.manual_schedule())
+
+        def tile(name, shape, dtype):
+            return sb.tile(shape, dtype, name=name, align_bytes=64)
+
+        def bank(name, tag):
+            return ps.tile([P, D], F32, name=name, tag=tag)
+
+        def load_words(queue, dst, src):
+            if len(src.shape) == 4:
+                rows = src[0].rearrange("p n r -> p (n r)")
+            else:
+                rows = src[0]
+            queue.dma_start(out=dst[:].bitcast(I32), in_=rows.bitcast(I32))
+
+        def load_scale_rows(queue, plane, src, r):
+            queue.dma_start(out=plane.bitcast(I32)[32 * r:32 * r + 4, :], in_=src[0].bitcast(I32)[4 * r:4 * r + 4, :])
+
+        xt_c = tile("xt_c", [P, D], U32)
+        wo_c = tile("wo_c", [P, D], U32)
+        wb_c = tile("wb_c", [P, D], U32)
+        wc_c = tile("wc_c", [P, 2 * D], U8)
+        wr_in = tile("wr_in", [P, 2 * D], U8)
+        wr_c = tile("wr_c", [P, 2 * D], U8)
+        xt_s = tile("xt_s", [P, D], U8)[:]
+        wc_s = tile("wc_s", [P, D], U8)[:]
+        wr_s_in = tile("wr_s_in", [P, D], U8)[:]
+        later_planes = tile("later_planes", [P, 2 * D], U8)
+        wo_s, wb_s = later_planes[:, 0:D], later_planes[:, D:2 * D]
+        wr_s = tile("wr_s", [P, D], U8)
+        fj_sb = tile("fj_sb", [P, R], F32)
+        fm_sb = tile("fm_sb", [P, R], F32)
+        tg_sb = [tile("tg%d" % h, [P, 2, D], F32) for h in range(2)]
+        tr_sb = [tile("tr%d" % h, [P, 2, D], F32) for h in range(2)]
+        ident = tile("ident", [P, P], F32)
+        warm = tile("warm", [P, 1], F32)
+        warm_out = tile("warm_out", [P, 1], F32)
+
+        for plane in (xt_s, wc_s, wr_s_in, later_planes[:]):
+            nc.gpsimd.memset(plane.bitcast(I32), 0)
+        nc.vector.memset(warm[:], 0.0)
+        nc.scalar.activation(out=warm_out[:], in_=warm[:], func=ACT.Exp)
+        make_identity(nc, ident[:])
+
+        tg_rows = tg.rearrange("(h i p) j -> h p i j", i=2, p=P)
+        tr_rows = tr1.rearrange("(p r) t -> p r t", r=R)
+        load_words(nc.sync, wc_c, wc_words)
+        load_words(nc.sync, xt_c, xt_words)
+        load_words(nc.sync, wr_in, wr_words)
+        for plane, src in ((xt_s, xt_scales), (wc_s, wc_scales), (wr_s_in, wr_scales)):
+            for q in range(4):
+                load_scale_rows(nc.sync, plane, src, q)
+        nc.sync.dma_start(out=fm_sb[:], in_=fm.rearrange("(p r) o -> p (r o)", r=R))
+        for h in range(2):
+            nc.sync.dma_start(out=tr_sb[h][:], in_=tr_rows[:, 2 * h:2 * h + 2, :])
+        nc.sync.dma_start(out=fj_sb[:], in_=fj.rearrange("(p r) o -> p (r o)", r=R))
+        for h in range(2):
+            nc.sync.dma_start(out=tg_sb[h][:], in_=tg_rows[h])
+        for words, src_words, plane, src in ((wb_c, wb_words, wb_s, wb_scales), (wo_c, wo_words, wo_s, wo_scales)):
+            for q in range(4):
+                load_scale_rows(nc.sync, plane, src, q)
+            load_words(nc.sync, words, src_words)
+
+        cols = [slice(i * P, (i + 1) * P) for i in range(NT)]
+        halves = [slice(h * HALF, (h + 1) * HALF) for h in range(2)]
+
+        scores = [bank("scores%d" % i, "low%d" % i) for i in range(NT)]
+        for i in range(NT):
+            nc.tensor.matmul_mx(
+                out=scores[i][:], lhsT=xt_c[:, cols[i]].bitcast(E4M3), lhsT_scale=xt_s[:, cols[i]],
+                rhs=wc_c[:].bitcast(E2M1), rhs_scale=wc_s, start=True, stop=True,
+            )
+
+        neg_max = [tile("neg_max%d" % i, [P, 1], F32) for i in range(NT)]
+        total = [tile("total%d" % i, [P, 1], F32) for i in range(NT)]
+        inv_total = [tile("inv_total%d" % i, [P, 1], F32) for i in range(NT)]
+        e_sb = [tile("e%d" % i, [P, D], F32) for i in range(NT)]
+        share = [tile("share%d" % i, [P, D], F32) for i in range(NT)]
+        neg_tg = [tile("neg_tg%d" % i, [P, D], F32) for i in range(NT)]
+        d_bank = {}
+        dj_bf = [tile("dj_bf%d" % i, [P, P * R], BF16) for i in range(NT)]
+        dj_c = tile("dj_c", [P, D], U32)
+        dj_s = tile("dj_s", [P, D], U8)
+        trf = [tile("trf%d" % r, [P, D], F32) for r in range(R)]
+        dm_rows = tile("dm_rows", [P, R, D], BF16)
+        dm_bf = [tile("dm_bf%d" % h, [P, HALF * R], BF16) for h in range(2)]
+        dm_c = tile("dm_c", [P, D], U32)
+        dm_s = tile("dm_s", [P, D], U8)
+        r_bank = {}
+        out_bank = {}
+
+        def row_max(i):
+            nc.vector.tensor_reduce(out=neg_max[i][:], in_=scores[i][:], axis=AX.X, op=ALU.max, negate=True)
+
+        def exponential(i):
+            nc.scalar.activation(
+                out=e_sb[i][:].rearrange("p (r m) -> p r m", r=R),
+                in_=scores[i][:].rearrange("p (m r) -> p r m", r=R),
+                func=ACT.Exp, bias=neg_max[i][:], accum_out=total[i][:],
+            )
+
+        def invert(i):
+            nc.vector.reciprocal(out=inv_total[i][:], in_=total[i][:])
+
+        def normalise_scalar(i):
+            nc.scalar.activation(out=share[i][:], in_=e_sb[i][:], func=ACT.Copy, scale=inv_total[i][:])
+
+        def normalise_vector(i):
+            nc.vector.tensor_scalar(
+                out=share[i][:], in0=e_sb[i][:], scalar1=inv_total[i][:], scalar2=None, op0=ALU.mult,
+            )
+
+        def negate_targets(i):
+            nc.gpsimd.tensor_scalar(
+                out=neg_tg[i][:].rearrange("p (r c u) -> p c r u", r=R, u=4),
+                in0=tg_sb[i // 2][:, i % 2, :].rearrange("p (c u r) -> p c r u", r=R, u=4),
+                scalar1=-1.0, scalar2=0.0, op0=ALU.mult, op1=ALU.add,
+            )
+
+        def transposes(i, src, first):
+            if first:
+                d_bank[i] = bank("d%d" % i, "low%d" % i)
+            for r in range(R):
+                nc.tensor.matmul(
+                    out=d_bank[i][:, cols[r]], lhsT=src[:, cols[r]], rhs=ident[:], is_transpose=True,
+                    start=(first and r == 0), stop=(not first and r == R - 1),
+                )
+
+        def class_error(i):
+            nc.vector.tensor_tensor(
+                out=dj_bf[i][:].rearrange("p (t r) -> p t r", r=R),
+                in0=d_bank[i][:].rearrange("p (r t) -> p t r", r=R),
+                in1=fj_sb[:].unsqueeze(1).to_broadcast([P, P, R]),
+                op=ALU.mult,
+            )
+
+        def quantise_dj(i):
+            nc.vector.quantize_mx(out=dj_c[:, cols[i]].bitcast(E5M2), scales=dj_s[:, cols[i]], in_=dj_bf[i][:])
+
+        def permute_wr():
+            nc.vector.tensor_copy(
+                out=wr_c[:].rearrange("p (r c u b) -> p c r u b", r=R, u=8, b=2),
+                in_=wr_in[:].rearrange("p (c u r b) -> p c r u b", r=R, u=8, b=2),
+            )
+            nc.vector.tensor_copy(
+                out=wr_s[:].rearrange("p (r c u) -> p c r u", r=R, u=16),
+                in_=wr_s_in.rearrange("p (c u r) -> p c r u", r=R, u=16),
+            )
+
+        def regression(r):
+            r_bank[r] = bank("r%d" % r, "high%d" % r)
+            nc.tensor.matmul_mx(
+                out=r_bank[r][:], lhsT=wr_c[:, 2 * P * r:2 * P * (r + 1)].bitcast(E2M1), lhsT_scale=wr_s[:, cols[r]],
+                rhs=xt_c[:].bitcast(E4M3), rhs_scale=xt_s, start=True, stop=True,
+            )
+
+        def scale_targets(r):
+            nc.gpsimd.tensor_scalar(
+                out=trf[r][:], in0=tr_sb[r // 2][:, r % 2, :],
+                scalar1=fm_sb[:, r:r + 1], scalar2=0.0, op0=ALU.mult, op1=ALU.add,
+            )
+
+        def regression_error(r):
+            nc.vector.scalar_tensor_tensor(
+                out=dm_rows[:, r, :], in0=r_bank[r][:], scalar=fm_sb[:, r:r + 1],
+                in1=trf[r][:], op0=ALU.mult, op1=ALU.subtract,
+            )
+
+        def interleave(i):
+            nc.scalar.copy(
+                out=dm_bf[i // 2][:, (i % 2) * D:(i % 2 + 1) * D].rearrange("p (c u r) -> p c r u", u=4, r=R),
+                in_=dm_rows[:, :, cols[i]].rearrange("p r (c u) -> p c r u", u=4),
+            )
+
+        def quantise_dm(h):
+            nc.vector.quantize_mx(out=dm_c[:, halves[h]].bitcast(E4M3), scales=dm_s[:, halves[h]], in_=dm_bf[h][:])
+
+        def back_regression(q):
+            out_bank[q] = bank("out%d" % q, "high%d" % q)
+            nc.tensor.matmul_mx(
+                out=out_bank[q][:], lhsT=wb_c[:, cols[q]].bitcast(E4M3), lhsT_scale=wb_s[:, cols[q]],
+                rhs=dm_c[:].bitcast(E4M3), rhs_scale=dm_s[:], start=True, stop=False,
+            )
+
+        def back_classes(q):
+            nc.tensor.matmul_mx(
+                out=out_bank[q][:], lhsT=wo_c[:, cols[q]].bitcast(E4M3), lhsT_scale=wo_s[:, cols[q]],
+                rhs=dj_c[:].bitcast(E5M2), rhs_scale=dj_s[:], start=False, stop=True,
+            )
+
+        permute_wr()
+        for r in range(R):
+            regression(r)
+        for r in range(R):
+            scale_targets(r)
+        for i in range(NT):
+            negate_targets(i)
+
+        for i in range(NT):
+            row_max(i)
+            exponential(i)
+            if i >= 2:
+                invert(i - 2)
+        normalise_scalar(0)
+        normalise_scalar(1)
+        regression_error(0)
+        invert(2)
+        regression_error(1)
+        invert(3)
+        regression_error(2)
+        regression_error(3)
+        normalise_vector(2)
+        normalise_vector(3)
+        for i in range(NT):
+            interleave(i)
+        transposes(0, share[0], True)
+        transposes(1, share[1], True)
+        transposes(0, neg_tg[0], False)
+        transposes(1, neg_tg[1], False)
+        for i in (2, 3):
+            transposes(i, share[i], True)
+            transposes(i, neg_tg[i], False)
+        class_error(0)
+        quantise_dm(0)
+        class_error(1)
+        quantise_dj(0)
+        quantise_dm(1)
+        quantise_dj(1)
+        class_error(2)
+        class_error(3)
+        quantise_dj(2)
+        quantise_dj(3)
+        for q in range(NT):
+            back_regression(q)
+        for q in range(NT):
+            back_classes(q)
+        for q in range(NT):
+            result = tile("result%d" % q, [P, D], F32)
+            if q % 2 == 0:
+                nc.scalar.copy(out=result[:], in_=out_bank[q][:])
+            else:
+                nc.vector.tensor_copy(out=result[:], in_=out_bank[q][:])
+            nc.sync.dma_start(out=out[cols[q], :], in_=result[:])

@@ -69,24 +69,30 @@ def tile_mix_errors_of_two_heads_back_kernel(
         warm = tile("warm", [P, 1], F32)
         warm_out = tile("warm_out", [P, 1], F32)
 
-        for plane in (xt_s, wc_s, wr_s_in, later_planes[:]):
-            nc.gpsimd.memset(plane.bitcast(I32), 0)
+        nc.vector.memset(xt_s.bitcast(I32), 0)
+        nc.gpsimd.memset(wc_s.bitcast(I32), 0)
         nc.vector.memset(warm[:], 0.0)
+        nc.vector.memset(wr_s_in.bitcast(I32), 0)
+        nc.vector.memset(later_planes[:].bitcast(I32), 0)
+        nc.gpsimd.dma_start(out=fm_sb[:], in_=fm.rearrange("(p r) o -> p (r o)", r=R))
+        nc.gpsimd.dma_start(out=fj_sb[:], in_=fj.rearrange("(p r) o -> p (r o)", r=R))
         nc.scalar.activation(out=warm_out[:], in_=warm[:], func=ACT.Exp)
         make_identity(nc, ident[:])
 
         tg_rows = tg.rearrange("(h i p) j -> h p i j", i=2, p=P)
         tr_rows = tr1.rearrange("(p r) t -> p r t", r=R)
         load_words(nc.sync, wc_c, wc_words)
+        for q in range(4):
+            load_scale_rows(nc.sync, xt_s, xt_scales, q)
+        load_scale_rows(nc.sync, wc_s, wc_scales, 0)
         load_words(nc.sync, xt_c, xt_words)
         load_words(nc.sync, wr_in, wr_words)
-        for plane, src in ((xt_s, xt_scales), (wc_s, wc_scales), (wr_s_in, wr_scales)):
-            for q in range(4):
-                load_scale_rows(nc.sync, plane, src, q)
-        nc.sync.dma_start(out=fm_sb[:], in_=fm.rearrange("(p r) o -> p (r o)", r=R))
-        for h in range(2):
-            nc.sync.dma_start(out=tr_sb[h][:], in_=tr_rows[:, 2 * h:2 * h + 2, :])
-        nc.sync.dma_start(out=fj_sb[:], in_=fj.rearrange("(p r) o -> p (r o)", r=R))
+        for q in range(1, 4):
+            load_scale_rows(nc.sync, wc_s, wc_scales, q)
+        nc.sync.dma_start(out=tr_sb[0][:], in_=tr_rows[:, 0:2, :])
+        for q in range(4):
+            load_scale_rows(nc.sync, wr_s_in, wr_scales, q)
+        nc.sync.dma_start(out=tr_sb[1][:], in_=tr_rows[:, 2:4, :])
         for h in range(2):
             nc.sync.dma_start(out=tg_sb[h][:], in_=tg_rows[h])
         for words, src_words, plane, src in ((wb_c, wb_words, wb_s, wb_scales), (wo_c, wo_words, wo_s, wo_scales)):
@@ -135,19 +141,16 @@ def tile_mix_errors_of_two_heads_back_kernel(
         def invert(i):
             nc.vector.reciprocal(out=inv_total[i][:], in_=total[i][:])
 
-        def normalise_scalar(i):
-            nc.scalar.activation(out=share[i][:], in_=e_sb[i][:], func=ACT.Copy, scale=inv_total[i][:])
-
-        def normalise_vector(i):
-            nc.vector.tensor_scalar(
-                out=share[i][:], in0=e_sb[i][:], scalar1=inv_total[i][:], scalar2=None, op0=ALU.mult,
+        def normalise(i):
+            nc.gpsimd.tensor_scalar(
+                out=share[i][:], in0=e_sb[i][:], scalar1=inv_total[i][:], scalar2=0.0, op0=ALU.mult, op1=ALU.add,
             )
 
         def negate_targets(i):
-            nc.gpsimd.tensor_scalar(
+            nc.scalar.activation(
                 out=neg_tg[i][:].rearrange("p (r c u) -> p c r u", r=R, u=4),
-                in0=tg_sb[i // 2][:, i % 2, :].rearrange("p (c u r) -> p c r u", r=R, u=4),
-                scalar1=-1.0, scalar2=0.0, op0=ALU.mult, op1=ALU.add,
+                in_=tg_sb[i // 2][:, i % 2, :].rearrange("p (c u r) -> p c r u", r=R, u=4),
+                func=ACT.Copy, scale=-1.0,
             )
 
         def transposes(i, src, first):
@@ -170,11 +173,13 @@ def tile_mix_errors_of_two_heads_back_kernel(
         def quantise_dj(i):
             nc.vector.quantize_mx(out=dj_c[:, cols[i]].bitcast(E5M2), scales=dj_s[:, cols[i]], in_=dj_bf[i][:])
 
-        def permute_wr():
+        def permute_wr_words():
             nc.vector.tensor_copy(
                 out=wr_c[:].rearrange("p (r c u b) -> p c r u b", r=R, u=8, b=2),
                 in_=wr_in[:].rearrange("p (c u r b) -> p c r u b", r=R, u=8, b=2),
             )
+
+        def permute_wr_scales():
             nc.vector.tensor_copy(
                 out=wr_s[:].rearrange("p (r c u) -> p c r u", r=R, u=16),
                 in_=wr_s_in.rearrange("p (c u r) -> p c r u", r=R, u=16),
@@ -199,8 +204,8 @@ def tile_mix_errors_of_two_heads_back_kernel(
                 in1=trf[r][:], op0=ALU.mult, op1=ALU.subtract,
             )
 
-        def interleave(i):
-            nc.scalar.copy(
+        def interleave(copy, i):
+            copy(
                 out=dm_bf[i // 2][:, (i % 2) * D:(i % 2 + 1) * D].rearrange("p (c u r) -> p c r u", u=4, r=R),
                 in_=dm_rows[:, :, cols[i]].rearrange("p r (c u) -> p c r u", u=4),
             )
@@ -221,45 +226,43 @@ def tile_mix_errors_of_two_heads_back_kernel(
                 rhs=dj_c[:].bitcast(E5M2), rhs_scale=dj_s[:], start=False, stop=True,
             )
 
-        permute_wr()
-        for r in range(R):
-            regression(r)
+        permute_wr_words()
         for r in range(R):
             scale_targets(r)
         for i in range(NT):
-            negate_targets(i)
-
-        for i in range(NT):
             row_max(i)
             exponential(i)
+            if i == 0:
+                permute_wr_scales()
+                for r in range(R):
+                    regression(r)
             if i >= 2:
                 invert(i - 2)
-        normalise_scalar(0)
-        normalise_scalar(1)
         regression_error(0)
         invert(2)
         regression_error(1)
         invert(3)
         regression_error(2)
         regression_error(3)
-        normalise_vector(2)
-        normalise_vector(3)
         for i in range(NT):
-            interleave(i)
-        transposes(0, share[0], True)
-        transposes(1, share[1], True)
-        transposes(0, neg_tg[0], False)
-        transposes(1, neg_tg[1], False)
-        for i in (2, 3):
-            transposes(i, share[i], True)
-            transposes(i, neg_tg[i], False)
+            normalise(i)
+        for i in range(3):
+            negate_targets(i)
+        interleave(nc.vector.tensor_copy, 0)
+        interleave(nc.scalar.copy, 1)
+        negate_targets(3)
+        interleave(nc.scalar.copy, 2)
+        interleave(nc.scalar.copy, 3)
+        for i in range(NT):
+            transposes(i, neg_tg[i], True)
+            transposes(i, share[i], False)
         class_error(0)
-        quantise_dm(0)
         class_error(1)
         quantise_dj(0)
-        quantise_dm(1)
+        quantise_dm(0)
         quantise_dj(1)
         class_error(2)
+        quantise_dm(1)
         class_error(3)
         quantise_dj(2)
         quantise_dj(3)

@@ -70,7 +70,7 @@ def tile_mix_errors_of_two_heads_back_kernel(
         warm_out = tile("warm_out", [P, 1], F32)
 
         nc.vector.memset(xt_s.bitcast(I32), 0)
-        nc.gpsimd.memset(wc_s.bitcast(I32), 0)
+        nc.vector.memset(wc_s.bitcast(I32), 0)
         nc.vector.memset(warm[:], 0.0)
         nc.vector.memset(wr_s_in.bitcast(I32), 0)
         nc.vector.memset(later_planes[:].bitcast(I32), 0)
@@ -84,11 +84,12 @@ def tile_mix_errors_of_two_heads_back_kernel(
         load_words(nc.sync, wc_c, wc_words)
         for q in range(4):
             load_scale_rows(nc.sync, xt_s, xt_scales, q)
-        load_scale_rows(nc.sync, wc_s, wc_scales, 0)
-        load_words(nc.sync, xt_c, xt_words)
-        load_words(nc.sync, wr_in, wr_words)
-        for q in range(1, 4):
+        for q in range(2):
             load_scale_rows(nc.sync, wc_s, wc_scales, q)
+        load_words(nc.sync, xt_c, xt_words)
+        for q in range(2, 4):
+            load_scale_rows(nc.sync, wc_s, wc_scales, q)
+        load_words(nc.sync, wr_in, wr_words)
         nc.sync.dma_start(out=tr_sb[0][:], in_=tr_rows[:, 0:2, :])
         for q in range(4):
             load_scale_rows(nc.sync, wr_s_in, wr_scales, q)
@@ -103,12 +104,15 @@ def tile_mix_errors_of_two_heads_back_kernel(
         cols = [slice(i * P, (i + 1) * P) for i in range(NT)]
         halves = [slice(h * HALF, (h + 1) * HALF) for h in range(2)]
 
-        scores = [bank("scores%d" % i, "low%d" % i) for i in range(NT)]
-        for i in range(NT):
+        def scores_pass(dst, i):
             nc.tensor.matmul_mx(
-                out=scores[i][:], lhsT=xt_c[:, cols[i]].bitcast(E4M3), lhsT_scale=xt_s[:, cols[i]],
+                out=dst[:], lhsT=xt_c[:, cols[i]].bitcast(E4M3), lhsT_scale=xt_s[:, cols[i]],
                 rhs=wc_c[:].bitcast(E2M1), rhs_scale=wc_s, start=True, stop=True,
             )
+
+        scores = [bank("scores%d" % i, "low%d" % i) for i in range(NT)]
+        for i in range(NT):
+            scores_pass(scores[i], i)
 
         neg_max = [tile("neg_max%d" % i, [P, 1], F32) for i in range(NT)]
         total = [tile("total%d" % i, [P, 1], F32) for i in range(NT)]
@@ -253,9 +257,15 @@ def tile_mix_errors_of_two_heads_back_kernel(
         negate_targets(3)
         interleave(nc.scalar.copy, 2)
         interleave(nc.scalar.copy, 3)
+        spare = bank("spare", "high0")
         for i in range(NT):
+            if i % 2 == 0:
+                scores_pass(spare, 0)
+                scores_pass(spare, 0)
             transposes(i, neg_tg[i], True)
             transposes(i, share[i], False)
+        scores_pass(spare, 0)
+        scores_pass(spare, 0)
         class_error(0)
         class_error(1)
         quantise_dj(0)

@@ -96,10 +96,12 @@ def tile_mix_errors_of_two_heads_back_kernel(
         nc.sync.dma_start(out=tr_sb[1][:], in_=tr_rows[:, 2:4, :])
         for h in range(2):
             nc.sync.dma_start(out=tg_sb[h][:], in_=tg_rows[h])
-        for words, src_words, plane, src in ((wb_c, wb_words, wb_s, wb_scales), (wo_c, wo_words, wo_s, wo_scales)):
-            for q in range(4):
-                load_scale_rows(nc.sync, plane, src, q)
-            load_words(nc.sync, words, src_words)
+            for q in (2 * h, 2 * h + 1):
+                load_scale_rows(nc.sync, wo_s, wo_scales, q)
+        load_words(nc.sync, wo_c, wo_words)
+        load_words(nc.sync, wb_c, wb_words)
+        for q in range(4):
+            load_scale_rows(nc.sync, wb_s, wb_scales, q)
 
         cols = [slice(i * P, (i + 1) * P) for i in range(NT)]
         halves = [slice(h * HALF, (h + 1) * HALF) for h in range(2)]
@@ -122,8 +124,10 @@ def tile_mix_errors_of_two_heads_back_kernel(
         neg_tg = [tile("neg_tg%d" % i, [P, D], F32) for i in range(NT)]
         d_bank = {}
         dj_bf = [tile("dj_bf%d" % i, [P, P * R], BF16) for i in range(NT)]
-        dj_c = tile("dj_c", [P, D], U32)
-        dj_s = tile("dj_s", [P, D], U8)
+        dj_c = tile("dj_c", [P, HALF + D], U32)
+        dj_s = tile("dj_s", [P, HALF + D], U8)
+        nc.vector.memset(dj_c[:, 0:HALF], 0)
+        nc.vector.memset(dj_s[:, 0:HALF].bitcast(I32), 0)
         trf = [tile("trf%d" % r, [P, D], F32) for r in range(R)]
         dm_rows = tile("dm_rows", [P, R, D], BF16)
         dm_bf = [tile("dm_bf%d" % h, [P, HALF * R], BF16) for h in range(2)]
@@ -175,7 +179,8 @@ def tile_mix_errors_of_two_heads_back_kernel(
             )
 
         def quantise_dj(i):
-            nc.vector.quantize_mx(out=dj_c[:, cols[i]].bitcast(E5M2), scales=dj_s[:, cols[i]], in_=dj_bf[i][:])
+            at = slice(HALF + i * P, HALF + (i + 1) * P)
+            nc.vector.quantize_mx(out=dj_c[:, at].bitcast(E5M2), scales=dj_s[:, at], in_=dj_bf[i][:])
 
         def permute_wr_words():
             nc.vector.tensor_copy(
@@ -217,18 +222,23 @@ def tile_mix_errors_of_two_heads_back_kernel(
         def quantise_dm(h):
             nc.vector.quantize_mx(out=dm_c[:, halves[h]].bitcast(E4M3), scales=dm_s[:, halves[h]], in_=dm_bf[h][:])
 
-        def back_regression(q):
-            out_bank[q] = bank("out%d" % q, "high%d" % q)
+        def back(h, q):
+            acc = bank("out%d%d" % (h, q), ("high%d", "low%d")[h] % q)
+            window = slice(h * HALF, h * HALF + D)
             nc.tensor.matmul_mx(
-                out=out_bank[q][:], lhsT=wb_c[:, cols[q]].bitcast(E4M3), lhsT_scale=wb_s[:, cols[q]],
-                rhs=dm_c[:].bitcast(E4M3), rhs_scale=dm_s[:], start=True, stop=False,
+                out=acc[:], lhsT=wo_c[:, cols[q]].bitcast(E4M3), lhsT_scale=wo_s[:, cols[q]],
+                rhs=dj_c[:, window].bitcast(E5M2), rhs_scale=dj_s[:, window], start=True, stop=False,
             )
+            nc.tensor.matmul_mx(
+                out=acc[:, halves[1]], lhsT=wb_c[:, cols[q]].bitcast(E4M3), lhsT_scale=wb_s[:, cols[q]],
+                rhs=dm_c[:, halves[h]].bitcast(E4M3), rhs_scale=dm_s[:, halves[h]], start=False, stop=True,
+            )
+            out_bank[h, q] = acc
 
-        def back_classes(q):
-            nc.tensor.matmul_mx(
-                out=out_bank[q][:], lhsT=wo_c[:, cols[q]].bitcast(E4M3), lhsT_scale=wo_s[:, cols[q]],
-                rhs=dj_c[:].bitcast(E5M2), rhs_scale=dj_s[:], start=False, stop=True,
-            )
+        def store(copy, h, q):
+            result = tile("result%d%d" % (h, q), [P, HALF], F32)
+            copy(out=result[:], in_=out_bank[h, q][:, halves[1]])
+            nc.sync.dma_start(out=out[cols[q], halves[h]], in_=result[:])
 
         permute_wr_words()
         for r in range(R):
@@ -264,26 +274,19 @@ def tile_mix_errors_of_two_heads_back_kernel(
                 scores_pass(spare, 0)
             transposes(i, neg_tg[i], True)
             transposes(i, share[i], False)
-        scores_pass(spare, 0)
-        scores_pass(spare, 0)
         class_error(0)
         class_error(1)
         quantise_dj(0)
         quantise_dm(0)
         quantise_dj(1)
+        for q in range(NT):
+            back(0, q)
+            store(nc.scalar.copy, 0, q)
         class_error(2)
         quantise_dm(1)
         class_error(3)
         quantise_dj(2)
         quantise_dj(3)
         for q in range(NT):
-            back_regression(q)
-        for q in range(NT):
-            back_classes(q)
-        for q in range(NT):
-            result = tile("result%d" % q, [P, D], F32)
-            if q % 2 == 0:
-                nc.scalar.copy(out=result[:], in_=out_bank[q][:])
-            else:
-                nc.vector.tensor_copy(out=result[:], in_=out_bank[q][:])
-            nc.sync.dma_start(out=out[cols[q], :], in_=result[:])
+            back(1, q)
+            store((nc.vector.tensor_copy, nc.scalar.copy)[q % 2], 1, q)

@@ -63,8 +63,14 @@ def tile_mix_errors_of_two_heads_back_kernel(
         wr_s = tile("wr_s", [P, D], U8)
         fj_sb = tile("fj_sb", [P, R], F32)
         fm_sb = tile("fm_sb", [P, R], F32)
-        tg_sb = [tile("tg%d" % h, [P, 2, D], F32) for h in range(2)]
-        tr_sb = [tile("tr%d" % h, [P, 2, D], F32) for h in range(2)]
+        tg_first = tile("tg_first", [P, D], F32)
+        tg_second = tile("tg_second", [P, D], F32)
+        tg_rest = tile("tg_rest", [P, 2, D], F32)
+        tg_sb = [tg_first[:], tg_second[:], tg_rest[:, 0, :], tg_rest[:, 1, :]]
+        tr_first = tile("tr_first", [P, D], F32)
+        tr_second = tile("tr_second", [P, D], F32)
+        tr_rest = tile("tr_rest", [P, 2, D], F32)
+        tr_sb = [tr_first[:], tr_second[:], tr_rest[:, 0, :], tr_rest[:, 1, :]]
         ident = tile("ident", [P, P], F32)
         warm = tile("warm", [P, 1], F32)
         warm_out = tile("warm_out", [P, 1], F32)
@@ -74,12 +80,13 @@ def tile_mix_errors_of_two_heads_back_kernel(
         nc.vector.memset(warm[:], 0.0)
         nc.vector.memset(wr_s_in.bitcast(I32), 0)
         nc.vector.memset(later_planes[:].bitcast(I32), 0)
+        load_words(nc.gpsimd, wr_in, wr_words)
         nc.gpsimd.dma_start(out=fm_sb[:], in_=fm.rearrange("(p r) o -> p (r o)", r=R))
         nc.gpsimd.dma_start(out=fj_sb[:], in_=fj.rearrange("(p r) o -> p (r o)", r=R))
         nc.scalar.activation(out=warm_out[:], in_=warm[:], func=ACT.Exp)
         make_identity(nc, ident[:])
 
-        tg_rows = tg.rearrange("(h i p) j -> h p i j", i=2, p=P)
+        tg_rows = tg.rearrange("(i p) j -> p i j", p=P)
         tr_rows = tr1.rearrange("(p r) t -> p r t", r=R)
         load_words(nc.sync, wc_c, wc_words)
         for q in range(4):
@@ -89,15 +96,16 @@ def tile_mix_errors_of_two_heads_back_kernel(
         load_words(nc.sync, xt_c, xt_words)
         for q in range(2, 4):
             load_scale_rows(nc.sync, wc_s, wc_scales, q)
-        load_words(nc.sync, wr_in, wr_words)
-        nc.sync.dma_start(out=tr_sb[0][:], in_=tr_rows[:, 0:2, :])
         for q in range(4):
             load_scale_rows(nc.sync, wr_s_in, wr_scales, q)
-        nc.sync.dma_start(out=tr_sb[1][:], in_=tr_rows[:, 2:4, :])
-        for h in range(2):
-            nc.sync.dma_start(out=tg_sb[h][:], in_=tg_rows[h])
-            for q in (2 * h, 2 * h + 1):
-                load_scale_rows(nc.sync, wo_s, wo_scales, q)
+        nc.sync.dma_start(out=tg_first[:], in_=tg_rows[:, 0, :])
+        nc.sync.dma_start(out=tr_first[:], in_=tr_rows[:, 0, :])
+        nc.sync.dma_start(out=tr_second[:], in_=tr_rows[:, 1, :])
+        nc.sync.dma_start(out=tr_rest[:], in_=tr_rows[:, 2:4, :])
+        nc.sync.dma_start(out=tg_second[:], in_=tg_rows[:, 1, :])
+        nc.sync.dma_start(out=tg_rest[:], in_=tg_rows[:, 2:4, :])
+        for q in range(4):
+            load_scale_rows(nc.sync, wo_s, wo_scales, q)
         load_words(nc.sync, wo_c, wo_words)
         load_words(nc.sync, wb_c, wb_words)
         for q in range(4):
@@ -154,10 +162,13 @@ def tile_mix_errors_of_two_heads_back_kernel(
                 out=share[i][:], in0=e_sb[i][:], scalar1=inv_total[i][:], scalar2=0.0, op0=ALU.mult, op1=ALU.add,
             )
 
+        def normalise_scalar(i):
+            nc.scalar.activation(out=share[i][:], in_=e_sb[i][:], func=ACT.Copy, scale=inv_total[i][:])
+
         def negate_targets(i):
             nc.scalar.activation(
                 out=neg_tg[i][:].rearrange("p (r c u) -> p c r u", r=R, u=4),
-                in_=tg_sb[i // 2][:, i % 2, :].rearrange("p (c u r) -> p c r u", r=R, u=4),
+                in_=tg_sb[i].rearrange("p (c u r) -> p c r u", r=R, u=4),
                 func=ACT.Copy, scale=-1.0,
             )
 
@@ -203,7 +214,7 @@ def tile_mix_errors_of_two_heads_back_kernel(
 
         def scale_targets(r):
             nc.gpsimd.tensor_scalar(
-                out=trf[r][:], in0=tr_sb[r // 2][:, r % 2, :],
+                out=trf[r][:], in0=tr_sb[r],
                 scalar1=fm_sb[:, r:r + 1], scalar2=0.0, op0=ALU.mult, op1=ALU.add,
             )
 
@@ -241,15 +252,15 @@ def tile_mix_errors_of_two_heads_back_kernel(
             nc.sync.dma_start(out=out[cols[q], halves[h]], in_=result[:])
 
         permute_wr_words()
+        permute_wr_scales()
+        for r in range(R):
+            regression(r)
+        negate_targets(0)
         for r in range(R):
             scale_targets(r)
         for i in range(NT):
             row_max(i)
             exponential(i)
-            if i == 0:
-                permute_wr_scales()
-                for r in range(R):
-                    regression(r)
             if i >= 2:
                 invert(i - 2)
         regression_error(0)
@@ -258,23 +269,31 @@ def tile_mix_errors_of_two_heads_back_kernel(
         invert(3)
         regression_error(2)
         regression_error(3)
-        for i in range(NT):
-            normalise(i)
-        for i in range(3):
-            negate_targets(i)
-        interleave(nc.vector.tensor_copy, 0)
+        normalise_scalar(0)
+        normalise(1)
+        normalise(2)
+        negate_targets(1)
+        negate_targets(2)
         interleave(nc.scalar.copy, 1)
+        normalise_scalar(3)
         negate_targets(3)
         interleave(nc.scalar.copy, 2)
         interleave(nc.scalar.copy, 3)
         spare = bank("spare", "high0")
-        for i in range(NT):
-            if i % 2 == 0:
-                scores_pass(spare, 0)
-                scores_pass(spare, 0)
-            transposes(i, neg_tg[i], True)
-            transposes(i, share[i], False)
+        transposes(0, neg_tg[0], True)
+        scores_pass(spare, 0)
+        scores_pass(spare, 0)
+        transposes(0, share[0], False)
+        transposes(1, neg_tg[1], True)
+        transposes(1, share[1], False)
+        scores_pass(spare, 0)
+        scores_pass(spare, 0)
+        transposes(2, neg_tg[2], True)
+        transposes(2, share[2], False)
+        transposes(3, share[3], True)
+        transposes(3, neg_tg[3], False)
         class_error(0)
+        interleave(nc.vector.tensor_copy, 0)
         class_error(1)
         quantise_dj(0)
         quantise_dm(0)
@@ -283,9 +302,9 @@ def tile_mix_errors_of_two_heads_back_kernel(
             back(0, q)
             store(nc.scalar.copy, 0, q)
         class_error(2)
-        quantise_dm(1)
         class_error(3)
         quantise_dj(2)
+        quantise_dm(1)
         quantise_dj(3)
         for q in range(NT):
             back(1, q)

from contextlib import ExitStack

import concourse.mybir as mybir
from concourse.masks import make_identity

F32 = mybir.dt.float32
BF16 = mybir.dt.bfloat16
I32 = mybir.dt.int32
U32 = mybir.dt.uint32
U8 = mybir.dt.uint8
E4M3 = mybir.dt.float8_e4m3fn_x4
E5M2 = mybir.dt.float8_e5m2_x4
E2M1 = mybir.dt.float4_e2m1fn_x4
ALU = mybir.AluOpType
ACT = mybir.ActivationFunctionType
AX = mybir.AxisListType

P = 128
D = 512
R = 4
NT = D // P
HALF = D // 2
FLOPS = 4 * 2 * D * D * D


def tile_mix_errors_of_two_heads_back_kernel(
    tc, xt_words, xt_scales, wc_words, wc_scales, tg, fj, wo_words, wo_scales,
    wr_words, wr_scales, tr1, fm, wb_words, wb_scales, out,
):
    nc = tc.nc
    with ExitStack() as ctx:
        sb = ctx.enter_context(tc.tile_pool(name="sb", bufs=1))
        ps = ctx.enter_context(tc.psum_pool(name="ps", bufs=1))
        ctx.enter_context(tc.manual_schedule())

        def tile(name, shape, dtype):
            return sb.tile(shape, dtype, name=name, align_bytes=64)

        def bank(name, tag):
            return ps.tile([P, D], F32, name=name, tag=tag)

        def load_words(queue, dst, src):
            if len(src.shape) == 4:
                rows = src[0].rearrange("p n r -> p (n r)")
            else:
                rows = src[0]
            queue.dma_start(out=dst[:].bitcast(I32), in_=rows.bitcast(I32))

        def load_scale_rows(queue, plane, src, r):
            queue.dma_start(out=plane.bitcast(I32)[32 * r:32 * r + 4, :], in_=src[0].bitcast(I32)[4 * r:4 * r + 4, :])

        xt_c = tile("xt_c", [P, D], U32)
        wo_c = tile("wo_c", [P, D], U32)
        wb_c = tile("wb_c", [P, D], U32)
        wc_c = tile("wc_c", [P, 2 * D], U8)
        wr_in = tile("wr_in", [P, 2 * D], U8)
        wr_c = tile("wr_c", [P, 2 * D], U8)
        xt_s = tile("xt_s", [P, D], U8)[:]
        wc_s = tile("wc_s", [P, D], U8)[:]
        wr_s_in = tile("wr_s_in", [P, D], U8)[:]
        later_planes = tile("later_planes", [P, 2 * D], U8)
        wo_s, wb_s = later_planes[:, 0:D], later_planes[:, D:2 * D]
        wr_s = tile("wr_s", [P, D], U8)
        fj_sb = tile("fj_sb", [P, R], F32)
        fm_sb = tile("fm_sb", [P, R], F32)
        tg_first = tile("tg_first", [P, D], F32)
        tg_second = tile("tg_second", [P, D], F32)
        tg_rest = tile("tg_rest", [P, 2, D], F32)
        tg_sb = [tg_first[:], tg_second[:], tg_rest[:, 0, :], tg_rest[:, 1, :]]
        tr_first = tile("tr_first", [P, D], F32)
        tr_second = tile("tr_second", [P, D], F32)
        tr_rest = tile("tr_rest", [P, 2, D], F32)
        tr_sb = [tr_first[:], tr_second[:], tr_rest[:, 0, :], tr_rest[:, 1, :]]
        ident = tile("ident", [P, P], F32)
        warm = tile("warm", [P, 1], F32)
        warm_out = tile("warm_out", [P, 1], F32)

        nc.vector.memset(xt_s.bitcast(I32), 0)
        nc.vector.memset(wc_s.bitcast(I32), 0)
        nc.vector.memset(warm[:], 0.0)
        nc.vector.memset(wr_s_in.bitcast(I32), 0)
        nc.vector.memset(later_planes[:].bitcast(I32), 0)
        load_words(nc.gpsimd, wr_in, wr_words)
        nc.gpsimd.dma_start(out=fm_sb[:], in_=fm.rearrange("(p r) o -> p (r o)", r=R))
        nc.gpsimd.dma_start(out=fj_sb[:], in_=fj.rearrange("(p r) o -> p (r o)", r=R))
        nc.scalar.activation(out=warm_out[:], in_=warm[:], func=ACT.Exp)
        make_identity(nc, ident[:])

        tg_rows = tg.rearrange("(i p) j -> p i j", p=P)
        tr_rows = tr1.rearrange("(p r) t -> p r t", r=R)
        load_words(nc.sync, wc_c, wc_words)
        for q in range(4):
            load_scale_rows(nc.sync, xt_s, xt_scales, q)
        for q in range(2):
            load_scale_rows(nc.sync, wc_s, wc_scales, q)
        load_words(nc.sync, xt_c, xt_words)
        for q in range(2, 4):
            load_scale_rows(nc.sync, wc_s, wc_scales, q)
        for q in range(4):
            load_scale_rows(nc.sync, wr_s_in, wr_scales, q)
        nc.sync.dma_start(out=tg_first[:], in_=tg_rows[:, 0, :])
        nc.sync.dma_start(out=tr_first[:], in_=tr_rows[:, 0, :])
        nc.sync.dma_start(out=tr_second[:], in_=tr_rows[:, 1, :])
        nc.sync.dma_start(out=tr_rest[:], in_=tr_rows[:, 2:4, :])
        nc.sync.dma_start(out=tg_second[:], in_=tg_rows[:, 1, :])
        nc.sync.dma_start(out=tg_rest[:], in_=tg_rows[:, 2:4, :])
        for q in range(4):
            load_scale_rows(nc.sync, wo_s, wo_scales, q)
        load_words(nc.sync, wo_c, wo_words)
        load_words(nc.sync, wb_c, wb_words)
        for q in range(4):
            load_scale_rows(nc.sync, wb_s, wb_scales, q)

        cols = [slice(i * P, (i + 1) * P) for i in range(NT)]
        halves = [slice(h * HALF, (h + 1) * HALF) for h in range(2)]

        def scores_pass(dst, i):
            nc.tensor.matmul_mx(
                out=dst[:], lhsT=xt_c[:, cols[i]].bitcast(E4M3), lhsT_scale=xt_s[:, cols[i]],
                rhs=wc_c[:].bitcast(E2M1), rhs_scale=wc_s, start=True, stop=True,
            )

        scores = [bank("scores%d" % i, "low%d" % i) for i in range(NT)]
        for i in range(NT):
            scores_pass(scores[i], i)

        neg_max = [tile("neg_max%d" % i, [P, 1], F32) for i in range(NT)]
        total = [tile("total%d" % i, [P, 1], F32) for i in range(NT)]
        inv_total = [tile("inv_total%d" % i, [P, 1], F32) for i in range(NT)]
        e_sb = [tile("e%d" % i, [P, D], F32) for i in range(NT)]
        share = [tile("share%d" % i, [P, D], F32) for i in range(NT)]
        neg_tg = [tile("neg_tg%d" % i, [P, D], F32) for i in range(NT)]
        d_bank = {}
        dj_bf = [tile("dj_bf%d" % i, [P, P * R], BF16) for i in range(NT)]
        dj_c = tile("dj_c", [P, HALF + D], U32)
        dj_s = tile("dj_s", [P, HALF + D], U8)
        nc.vector.memset(dj_c[:, 0:HALF], 0)
        nc.vector.memset(dj_s[:, 0:HALF].bitcast(I32), 0)
        trf = [tile("trf%d" % r, [P, D], F32) for r in range(R)]
        dm_rows = tile("dm_rows", [P, R, D], BF16)
        dm_bf = [tile("dm_bf%d" % h, [P, HALF * R], BF16) for h in range(2)]
        dm_c = tile("dm_c", [P, D], U32)
        dm_s = tile("dm_s", [P, D], U8)
        r_bank = {}
        out_bank = {}

        def row_max(i):
            nc.vector.tensor_reduce(out=neg_max[i][:], in_=scores[i][:], axis=AX.X, op=ALU.max, negate=True)

        def exponential(i):
            nc.scalar.activation(
                out=e_sb[i][:].rearrange("p (r m) -> p r m", r=R),
                in_=scores[i][:].rearrange("p (m r) -> p r m", r=R),
                func=ACT.Exp, bias=neg_max[i][:], accum_out=total[i][:],
            )

        def invert(i):
            nc.vector.reciprocal(out=inv_total[i][:], in_=total[i][:])

        def normalise(i):
            nc.gpsimd.tensor_scalar(
                out=share[i][:], in0=e_sb[i][:], scalar1=inv_total[i][:], scalar2=0.0, op0=ALU.mult, op1=ALU.add,
            )

        def normalise_scalar(i):
            nc.scalar.activation(out=share[i][:], in_=e_sb[i][:], func=ACT.Copy, scale=inv_total[i][:])

        def negate_targets(i):
            nc.scalar.activation(
                out=neg_tg[i][:].rearrange("p (r c u) -> p c r u", r=R, u=4),
                in_=tg_sb[i].rearrange("p (c u r) -> p c r u", r=R, u=4),
                func=ACT.Copy, scale=-1.0,
            )

        def transposes(i, src, first):
            if first:
                d_bank[i] = bank("d%d" % i, "low%d" % i)
            for r in range(R):
                nc.tensor.matmul(
                    out=d_bank[i][:, cols[r]], lhsT=src[:, cols[r]], rhs=ident[:], is_transpose=True,
                    start=(first and r == 0), stop=(not first and r == R - 1),
                )

        def class_error(i):
            nc.vector.tensor_tensor(
                out=dj_bf[i][:].rearrange("p (t r) -> p t r", r=R),
                in0=d_bank[i][:].rearrange("p (r t) -> p t r", r=R),
                in1=fj_sb[:].unsqueeze(1).to_broadcast([P, P, R]),
                op=ALU.mult,
            )

        def quantise_dj(i):
            at = slice(HALF + i * P, HALF + (i + 1) * P)
            nc.vector.quantize_mx(out=dj_c[:, at].bitcast(E5M2), scales=dj_s[:, at], in_=dj_bf[i][:])

        def permute_wr_words():
            nc.vector.tensor_copy(
                out=wr_c[:].rearrange("p (r c u b) -> p c r u b", r=R, u=8, b=2),
                in_=wr_in[:].rearrange("p (c u r b) -> p c r u b", r=R, u=8, b=2),
            )

        def permute_wr_scales():
            nc.vector.tensor_copy(
                out=wr_s[:].rearrange("p (r c u) -> p c r u", r=R, u=16),
                in_=wr_s_in.rearrange("p (c u r) -> p c r u", r=R, u=16),
            )

        def regression(r):
            r_bank[r] = bank("r%d" % r, "high%d" % r)
            nc.tensor.matmul_mx(
                out=r_bank[r][:], lhsT=wr_c[:, 2 * P * r:2 * P * (r + 1)].bitcast(E2M1), lhsT_scale=wr_s[:, cols[r]],
                rhs=xt_c[:].bitcast(E4M3), rhs_scale=xt_s, start=True, stop=True,
            )

        def scale_targets(r):
            nc.gpsimd.tensor_scalar(
                out=trf[r][:], in0=tr_sb[r],
                scalar1=fm_sb[:, r:r + 1], scalar2=0.0, op0=ALU.mult, op1=ALU.add,
            )

        def regression_error(r):
            nc.vector.scalar_tensor_tensor(
                out=dm_rows[:, r, :], in0=r_bank[r][:], scalar=fm_sb[:, r:r + 1],
                in1=trf[r][:], op0=ALU.mult, op1=ALU.subtract,
            )

        def interleave(copy, i):
            copy(
                out=dm_bf[i // 2][:, (i % 2) * D:(i % 2 + 1) * D].rearrange("p (c u r) -> p c r u", u=4, r=R),
                in_=dm_rows[:, :, cols[i]].rearrange("p r (c u) -> p c r u", u=4),
            )

        def quantise_dm(h):
            nc.vector.quantize_mx(out=dm_c[:, halves[h]].bitcast(E4M3), scales=dm_s[:, halves[h]], in_=dm_bf[h][:])

        def back(h, q):
            acc = bank("out%d%d" % (h, q), ("high%d", "low%d")[h] % q)
            window = slice(h * HALF, h * HALF + D)
            nc.tensor.matmul_mx(
                out=acc[:], lhsT=wo_c[:, cols[q]].bitcast(E4M3), lhsT_scale=wo_s[:, cols[q]],
                rhs=dj_c[:, window].bitcast(E5M2), rhs_scale=dj_s[:, window], start=True, stop=False,
            )
            nc.tensor.matmul_mx(
                out=acc[:, halves[1]], lhsT=wb_c[:, cols[q]].bitcast(E4M3), lhsT_scale=wb_s[:, cols[q]],
                rhs=dm_c[:, halves[h]].bitcast(E4M3), rhs_scale=dm_s[:, halves[h]], start=False, stop=True,
            )
            out_bank[h, q] = acc

        def store(copy, h, q):
            result = tile("result%d%d" % (h, q), [P, HALF], F32)
            copy(out=result[:], in_=out_bank[h, q][:, halves[1]])
            nc.sync.dma_start(out=out[cols[q], halves[h]], in_=result[:])

        permute_wr_words()
        permute_wr_scales()
        for r in range(R):
            regression(r)
        negate_targets(0)
        for r in range(R):
            scale_targets(r)
        for i in range(NT):
            row_max(i)
            exponential(i)
            if i >= 2:
                invert(i - 2)
        regression_error(0)
        invert(2)
        regression_error(1)
        invert(3)
        regression_error(2)
        regression_error(3)
        normalise_scalar(0)
        normalise(1)
        normalise(2)
        negate_targets(1)
        negate_targets(2)
        interleave(nc.scalar.copy, 1)
        normalise_scalar(3)
        negate_targets(3)
        interleave(nc.scalar.copy, 2)
        interleave(nc.scalar.copy, 3)
        spare = bank("spare", "high0")
        transposes(0, neg_tg[0], True)
        scores_pass(spare, 0)
        scores_pass(spare, 0)
        transposes(0, share[0], False)
        transposes(1, neg_tg[1], True)
        transposes(1, share[1], False)
        scores_pass(spare, 0)
        scores_pass(spare, 0)
        transposes(2, neg_tg[2], True)
        transposes(2, share[2], False)
        transposes(3, share[3], True)
        transposes(3, neg_tg[3], False)
        class_error(0)
        interleave(nc.vector.tensor_copy, 0)
        class_error(1)
        quantise_dj(0)
        quantise_dm(0)
        quantise_dj(1)
        for q in range(NT):
            back(0, q)
            store(nc.scalar.copy, 0, q)
        class_error(2)
        class_error(3)
        quantise_dj(2)
        quantise_dm(1)
        quantise_dj(3)
        for q in range(NT):
            back(1, q)
            store((nc.vector.tensor_copy, nc.scalar.copy)[q % 2], 1, q)
